import numpy as np
import ml_dtypes


def mxq(x, axis, fmt="e4m3"):
    dtype, down = {"e4m3": (ml_dtypes.float8_e4m3fn, 7), "e5m2": (ml_dtypes.float8_e5m2, 14)}[fmt]
    v = np.moveaxis(np.asarray(x, np.float32).astype(ml_dtypes.bfloat16).astype(np.float64), axis, -1)
    blocks = v.reshape(v.shape[:-1] + (-1, 32))
    amax = np.abs(blocks).max(-1, keepdims=True)
    byte = np.maximum(np.where(amax > 0, np.frexp(amax)[1] - 1 + 127, 0) - down, 1)
    scale = np.exp2(byte - 127.0)
    codes = (blocks / scale).astype(np.float32).astype(dtype).astype(np.float64)
    return np.moveaxis((codes * scale).reshape(v.shape), -1, axis)


WIDE = False


def mx_kscale(k):
    if not WIDE:
        return np.ones(k)
    levels = np.array([10, -10, 5, -5, 0])
    if k % 512:
        return np.exp2(np.random.permutation(np.resize(levels, k // 32))).repeat(32)
    a = np.empty((k // 512, 16))
    for p in range(k // 512):
        a[p, :8] = np.random.permutation(np.resize(levels, 8))
        for g in range(8):
            far = levels[np.abs(levels - a[p, g]) >= 10]
            a[p, g + 8] = far[np.random.randint(len(far))]
    return np.exp2(a.ravel()).repeat(32)


def f64(x):
    return np.asarray(x).astype(np.float64)


def striped(idx):
    return np.tile(idx.reshape(-1, 16).T, (8, 1)).astype(np.uint16)


def unstriped(offs):
    return offs[:16].T.reshape(-1).astype(np.int64)


E2M1 = np.array([0.0, 0.5, 1.0, 1.5, 2.0, 3.0, 4.0, 6.0, -0.0, -0.5, -1.0, -1.5, -2.0, -3.0, -4.0, -6.0])


def pack_weight(w, fmt):
    k, n = w.shape
    w = f64(np.asarray(w, np.float32).astype(ml_dtypes.bfloat16)).reshape(k // 32, 32, n)
    amax = np.abs(w).max(1)
    if fmt == "e4m3":
        byte = np.frexp(amax)[1] - 1 + 127 - 7
    else:
        mant, ex = np.frexp(amax / 6.0)
        byte = np.where(mant > 0.5, ex, ex - 1) + 127
    byte = np.clip(np.where(amax > 0, byte, 1), 1, 254)
    scaled = (w * np.exp2(127.0 - byte)[:, None, :]).reshape(k, n).astype(np.float32)
    by_word = np.ascontiguousarray(scaled.reshape(k // 512, 128, 4, n).transpose(0, 1, 3, 2))
    if fmt == "e4m3":
        words = by_word.astype(ml_dtypes.float8_e4m3fn).view(np.uint8)
    else:
        c = by_word.astype(ml_dtypes.float4_e2m1fn).view(np.uint8) & 0xF
        words = (c[..., 0::2] | (c[..., 1::2] << 4)).reshape(k // 512, 128, 2 * n)
    return np.ascontiguousarray(words), np.ascontiguousarray(byte.astype(np.uint8).reshape(k // 512, 16, n))


def unpack_weight(words, scales, fmt):
    g, _, n = scales.shape
    words = np.ascontiguousarray(words).reshape(g, 128, n, -1)
    if fmt == "e4m3":
        vals = words.view(ml_dtypes.float8_e4m3fn).astype(np.float64)
    else:
        nib = np.empty((g, 128, n, 4), np.uint8)
        nib[..., 0::2] = words & 0xF
        nib[..., 1::2] = words >> 4
        vals = E2M1[nib]
    vals = vals * np.repeat(np.exp2(scales.astype(np.float64) - 127.0), 8, axis=1)[..., None]
    return vals.transpose(0, 1, 3, 2).reshape(g * 512, n)


def gelu(v):
    return 0.5 * v * (1.0 + np.tanh(np.sqrt(2.0 / np.pi) * (v + 0.044715 * v**3)))


def bf(x):
    return np.asarray(x, np.float32).astype(ml_dtypes.bfloat16)


def planes(Y):
    n, m = Y.shape
    b = f64(bf(Y)).reshape(n // 32, 32, m)
    amax = np.abs(b).max(1)
    byte = np.clip(np.where(amax > 0, np.frexp(amax)[1] - 1 + 127 - 7, 1), 1, 254)
    codes = (b * np.exp2(127.0 - byte)[:, None, :]).reshape(n, m).astype(np.float32).astype(ml_dtypes.float8_e4m3fn).view(np.uint8)
    words = codes.reshape(n // 512, 128, 4, m).transpose(0, 1, 3, 2)
    return np.ascontiguousarray(words), np.ascontiguousarray(byte.astype(np.uint8).reshape(n // 512, 16, m))


K, T, S, P, P2, H, N = 512, 4096, 1024, 512, 256, 1024, 512


def setup_inputs():
    n = np.random.standard_normal
    s = mx_kscale(K)[:, None]
    u = mx_kscale(H)[:, None]
    size = np.exp(0.8 * n(N))[None, :]
    tab_words, tab_scales = pack_weight(n((K, T)) * s, "e4m3")
    w2_words, w2_scales = pack_weight(n((K, H)) * 0.8 / np.sqrt(K) / s, "e2m1")
    w4_words, w4_scales = pack_weight(n((H, N)) * size / np.sqrt(H) / u, "e2m1")
    w5_words, w5_scales = pack_weight(n((K, N)) * 0.8 * size / np.sqrt(K) / s, "e4m3")
    bays = np.random.permutation(P)
    return {
        "tab_words": tab_words, "tab_scales": tab_scales,
        "offs": striped(np.random.permutation(T)[:S]),
        "pos1": striped(np.random.permutation(S)[:P]),
        "pos2": striped(np.random.permutation(S)[:P]),
        "pos3": striped(bays[:P2]),
        "pos4": striped(bays[P2:]),
        "w1": (n((K, H)) * 1.6 / np.sqrt(K) / s).astype(np.float32),
        "w2_words": w2_words, "w2_scales": w2_scales,
        "gain": (np.exp(0.3 * n(H)) * np.sqrt(u[:, 0])).astype(np.float32),
        "w3": (n((H, N)) * size / np.sqrt(H) / u).astype(np.float32),
        "w4_words": w4_words, "w4_scales": w4_scales,
        "w5_words": w5_words, "w5_scales": w5_scales,
    }


def reference(tab_words, tab_scales, offs, pos1, pos2, pos3, pos4, w1, w2_words, w2_scales, gain, w3, w4_words, w4_scales, w5_words, w5_scales):
    v = unpack_weight(tab_words, tab_scales, "e4m3")[:, unstriped(offs)]
    l1, l2, l3, l4 = unstriped(pos1), unstriped(pos2), unstriped(pos3), unstriped(pos4)
    bent = np.tanh(mxq(f64(w1), 0, "e4m3").T @ v)
    h = f64(gain)[:, None] * (bent + (unpack_weight(w2_words, w2_scales, "e2m1").T @ v))
    zq = mxq(h[:, l1] * h[:, l2], 0, "e4m3")
    first = mxq(f64(w3), 0, "e4m3").T @ zq
    second = unpack_weight(w4_words, w4_scales, "e2m1").T @ zq
    skip = unpack_weight(w5_words, w5_scales, "e4m3").T @ v
    bloom = np.maximum(first, second) + skip[:, l1]
    y = bloom[:, l3] - bloom[:, l4]
    words, scales = planes(y)
    return y, words, scales

@@ -1,0 +1,333 @@
+from contextlib import ExitStack
+
+import concourse.mybir as mybir
+
+K, T, S, NPAIR, NCON, H, N = 512, 4096, 1024, 512, 256, 1024, 512
+FLOPS = 2 * (2 * K * H * S + 2 * H * N * NPAIR + K * N * S)
+
+F32 = mybir.dt.float32
+BF16 = mybir.dt.bfloat16
+I32 = mybir.dt.int32
+U32 = mybir.dt.uint32
+U16 = mybir.dt.uint16
+U8 = mybir.dt.uint8
+FP8X4 = mybir.dt.float8_e4m3fn_x4
+FP4X4 = mybir.dt.float4_e2m1fn_x4
+ALU = mybir.AluOpType
+ACT = mybir.ActivationFunctionType
+
+P = 128
+BLOCK = 512
+HALF = NPAIR // 2
+
+
+def tile_list_bloom_bay_contrast_kernel(
+    tc, tab_words, tab_scales, offs, pos1, pos2, pos3, pos4, w1, w2_words, w2_scales, gain, w3,
+    w4_words, w4_scales, w5_words, w5_scales, out_0, out_1, out_2,
+):
+    nc = tc.nc
+    with ExitStack() as ctx:
+        lists = ctx.enter_context(tc.tile_pool(name="lists", bufs=1))
+        keep = ctx.enter_context(tc.tile_pool(name="keep", bufs=1))
+        ring = ctx.enter_context(tc.tile_pool(name="ring", bufs=2))
+        psum = ctx.enter_context(tc.psum_pool(name="psum", bufs=1))
+
+        def held(shape, dtype, name, tag=None):
+            return keep.tile(shape, dtype, name=name, tag=tag or name, align_bytes=64)
+
+        def bank(i, name):
+            return psum.tile([P, BLOCK], F32, name=name, tag="bank%d" % i)
+
+        def load_list(src, name):
+            tile = lists.tile(list(src.shape), U16, name=name)
+            nc.sync.dma_start(tile[:], src)
+            return tile
+
+        def load_scale_rows(queue, tile, src, first_row):
+            passes, cols = src.shape[0], src.shape[2]
+            rows = src.bitcast(I32)
+            for q in range(4):
+                dst = tile[32 * q + first_row : 32 * q + first_row + 4, 0 : passes * cols].bitcast(I32)
+                queue.dma_start(
+                    dst.rearrange("r (a c) -> r a c", a=passes),
+                    rows[:, 4 * q : 4 * q + 4, :].rearrange("a r c -> r a c"),
+                )
+
+        def load_rows(src, name, tag):
+            tile = held([P, 4, BLOCK], F32, name, tag)
+            nc.sync.dma_start(tile[:], src.rearrange("(p j) c -> p j c", j=4))
+            return tile
+
+        def deal(dst, src):
+            nc.vector.tensor_copy(
+                dst.rearrange("p (b t m) -> p b t m", t=4, m=P),
+                src.rearrange("p (b m t) -> p b t m", t=4, m=P),
+            )
+
+        def round_weight(copy, raw, pair, name):
+            out = ring.tile([P, 2 * BLOCK], BF16, name=name, tag="rounded", bufs=3, align_bytes=64)
+            copy(
+                out[:].rearrange("p (t m j) -> p m t j", t=2, j=4),
+                raw[:].rearrange("p j (m t) -> p m t j", t=4)[:, :, 2 * pair : 2 * pair + 2, :],
+            )
+            return out
+
+        def quantise(src, name):
+            cols = src.shape[1] // 4
+            codes = held([P, cols], U32, name + "_codes")
+            scales = held([P, cols], U8, name + "_scales")
+            nc.vector.quantize_mx(out=codes[:].bitcast(FP8X4), scales=scales[:], in_=src[:])
+            return codes, scales
+
+        def interleave(copy, src, name):
+            cols = src.shape[2]
+            out = held([P, 4 * cols], BF16, name)
+            copy(
+                out[:].rearrange("p (c i t) -> p c t i", i=4, t=4),
+                src[:].rearrange("p t (c i) -> p c t i", i=4),
+            )
+            return out
+
+        offs_t = load_list(offs, "offs_t")
+        pos1_t = load_list(pos1, "pos1_t")
+        pos2_t = load_list(pos2, "pos2_t")
+        pos3_t = load_list(pos3, "pos3_t")
+        w2_raw = held([P, 2 * H], U8, "w2_raw", "stage_a")
+        nc.sync.dma_start(w2_raw[:].bitcast(I32), w2_words[0].bitcast(I32))
+        w1_raw = [load_rows(w1[:, 0:BLOCK], "w1_raw0", "stage_b")]
+        tabw = held([P, T], U32, "tabw")
+        nc.sync.dma_start(tabw[:].bitcast(I32), tab_words[0].rearrange("p n i -> p (n i)").bitcast(I32))
+        pos4_t = load_list(pos4, "pos4_t")
+
+        tabs = held([P, T], U8, "tabs")
+        nc.vector.memset(tabs[:].bitcast(I32), 0)
+        load_scale_rows(nc.scalar, tabs, tab_scales, 0)
+
+        gain_t = held([P, 2, 4], F32, "gain_t", "stage_d")
+        nc.gpsimd.dma_start(gain_t[:], gain.rearrange("(b p t) -> p b t", p=P, t=4))
+        w2s_raw = held([P, H], U8, "w2s_raw", "stage_c")
+        nc.gpsimd.memset(w2s_raw[:].bitcast(I32), 0)
+        load_scale_rows(nc.gpsimd, w2s_raw, w2_scales, 0)
+
+        widths = (NPAIR, HALF)
+        gain2 = []
+        for b in range(2):
+            g = held([P, 4, widths[b]], F32, "gain2_%d" % b)
+            nc.scalar.activation(g[:], gain_t[:, b, :].unsqueeze(2).to_broadcast([P, 4, widths[b]]), ACT.Square)
+            gain2.append(g)
+
+        w2c = held([P, 2 * H], U8, "w2c")
+        deal(w2c[:].bitcast(U16), w2_raw[:].bitcast(U16))
+        w1q = {}
+        r0 = round_weight(nc.vector.tensor_copy, w1_raw[0], 0, "w1r00")
+        r1 = round_weight(nc.scalar.copy, w1_raw[0], 1, "w1r01")
+        w1q[0, 0] = quantise(r0, "w1q00")
+
+        vs = held([P, S], U8, "vs")
+        nc.vector.tensor_copy(vs[:], tabs[:].indirect(offs_t[:]))
+        w2s = held([P, H], U8, "w2s")
+        deal(w2s[:], w2s_raw[:])
+        vw = []
+        for c in range(2):
+            v = held([P, BLOCK], U32, "vw%d" % c)
+            nc.vector.tensor_copy(v[:], tabw[:].indirect(offs_t[:, 32 * c : 32 * (c + 1)]))
+            vw.append(v)
+        w1q[0, 1] = quantise(r1, "w1q01")
+
+        w1_raw.append(load_rows(w1[:, BLOCK:H], "w1_raw1", "stage_a"))
+        w45_raw = held([P, 4 * N + 4 * N], U8, "w45_raw", "stage_d")
+        nc.sync.dma_start(w45_raw[:, 0 : 4 * N].bitcast(I32), w5_words[0].rearrange("p n i -> p (n i)").bitcast(I32))
+        nc.sync.dma_start(
+            w45_raw[:, 4 * N : 8 * N].bitcast(I32).rearrange("p (a c) -> p a c", a=2),
+            w4_words.bitcast(I32).rearrange("a p c -> p a c"),
+        )
+        w45s_raw = held([P, 2 * N], U8, "w45s_raw", "stage_c")
+        nc.gpsimd.memset(w45s_raw[:].bitcast(I32), 0)
+        load_scale_rows(nc.sync, w45s_raw, w5_scales, 4)
+        load_scale_rows(nc.sync, w45s_raw, w4_scales, 0)
+        w3_raw = [load_rows(w3[0:BLOCK, :], "w3_raw0", "stage_b"), load_rows(w3[BLOCK:H, :], "w3_raw1", "stage_a")]
+
+        def table_product(out, codes, scales, c):
+            nc.tensor.matmul_mx(
+                out=out[:], lhsT=codes, lhsT_scale=scales, rhs=vw[c][:].bitcast(FP8X4),
+                rhs_scale=vs[:, BLOCK * c : BLOCK * (c + 1)], start=True, stop=True,
+            )
+
+        u = [held([P, S], F32, "u%d" % s) for s in range(8)]
+        pending = {}
+
+        def first_products(s, c):
+            b, t = divmod(s, 4)
+            codes, scales = w1q[b, t // 2]
+            cols = slice(P * (t % 2), P * (t % 2 + 1))
+            acc1 = bank(c, "acc1_%d_%d" % (s, c))
+            table_product(acc1, codes[:, cols].bitcast(FP8X4), scales[:, cols], c)
+            acc2 = bank(2 + 2 * (s % 2) + c, "acc2_%d_%d" % (s, c))
+            table_product(acc2, w2c[:, 2 * P * s : 2 * P * (s + 1)].bitcast(FP4X4), w2s[:, P * s : P * (s + 1)], c)
+            bent = ring.tile([P, BLOCK], F32, name="bent%d_%d" % (s, c), tag="bent", bufs=4)
+            nc.scalar.activation(bent[:], acc1[:], ACT.Tanh)
+            pending[s, c] = (acc2, bent)
+
+        def add_products(s, c):
+            acc2, bent = pending[s, c]
+            nc.vector.tensor_tensor(u[s][:, BLOCK * c : BLOCK * (c + 1)], acc2[:], bent[:], ALU.add)
+
+        def pick_first(s, first, count):
+            b, t = divmod(s, 4)
+            a = ring.tile([P, count], F32, name="left%d_%d" % (s, first), tag="left", bufs=2)
+            idx = pos1_t[:, first // 16 : (first + count) // 16]
+            nc.vector.tensor_tensor(a[:], u[s][:].indirect(idx), gain2[b][:, t, :], ALU.mult)
+            return a
+
+        def pick_second(s, first, count, a, prod):
+            idx = pos2_t[:, first // 16 : (first + count) // 16]
+            nc.vector.tensor_tensor(prod[:, s % 4, :], u[s][:].indirect(idx), a[:], ALU.mult)
+
+        skip = [held([P, S], F32, "skip%d" % t) for t in range(4)]
+        w5c = held([P, N], U32, "w5c")
+        w4c = held([P, 4 * N], U8, "w4c")
+        w45s = held([P, 2 * N], U8, "w45s")
+
+        def deal_w45():
+            nc.vector.tensor_copy(
+                w5c[:].bitcast(I32).rearrange("p (t q i) -> p q t i", t=4, i=4),
+                w45_raw[:, 0 : 4 * N].bitcast(I32).rearrange("p (q i t) -> p q t i", t=4, i=4),
+            )
+            deal(w45s[:], w45s_raw[:])
+            deal(w4c[:].bitcast(U16), w45_raw[:, 4 * N : 8 * N].bitcast(U16))
+
+        def skip_product(t):
+            for c in range(2):
+                acc = bank(6 + c, "acc5_%d_%d" % (t, c))
+                table_product(acc, w5c[:, P * t : P * (t + 1)].bitcast(FP8X4), w45s[4:P, P * t : P * (t + 1)], c)
+                nc.scalar.copy(skip[t][:, BLOCK * c : BLOCK * (c + 1)], acc[:])
+
+        w3q = {}
+        prod0 = held([P, 4, NPAIR], F32, "prod0")
+        prod1 = [held([P, 4, HALF], F32, "prod1_%d" % e) for e in range(2)]
+        zq = {}
+
+        first_products(0, 0)
+        first_products(0, 1)
+        add_products(0, 0)
+        first_products(1, 0)
+        add_products(0, 1)
+        first_products(1, 1)
+        add_products(1, 0)
+        for s in range(8):
+            b = s // 4
+            a = pick_first(s, 0, widths[b])
+            if s + 1 < 8:
+                add_products(s + 1, 1)
+            if s + 2 < 8:
+                first_products(s + 2, 0)
+                first_products(s + 2, 1)
+            pick_second(s, 0, widths[b], a, prod0 if b == 0 else prod1[0])
+            if s + 2 < 8:
+                add_products(s + 2, 0)
+            if s == 0:
+                r0 = round_weight(nc.scalar.copy, w1_raw[1], 0, "w1r10")
+                r1 = round_weight(nc.scalar.copy, w1_raw[1], 1, "w1r11")
+                w1q[1, 0] = quantise(r0, "w1q10")
+                w1q[1, 1] = quantise(r1, "w1q11")
+            if s == 1:
+                deal_w45()
+            if 2 <= s < 6:
+                e = s - 2
+                w3q[divmod(e, 2)] = quantise(
+                    round_weight(nc.scalar.copy, w3_raw[e // 2], e % 2, "w3r%d" % e), "w3q%d" % e
+                )
+                skip_product(e)
+            if s == 3:
+                z0 = interleave(nc.scalar.copy, prod0, "z0")
+            if s == 4:
+                zq[0] = quantise(z0, "zq0")
+
+        bloom = [held([P, NPAIR], F32, "bloom%d" % t) for t in range(4)]
+        sums = {}
+        banks_of = ((6, 7, 0, 1), (2, 3, 4, 5))
+
+        def second_pass(e, g, a):
+            if a == 0:
+                sums[e, g] = (bank(banks_of[e][g], "acc3_%d_%d" % (e, g)), bank(banks_of[e][2 + g], "acc4_%d_%d" % (e, g)))
+                codes, scales = zq[0]
+                cols = slice(HALF * e, HALF * (e + 1))
+            else:
+                codes, scales = zq[1, e]
+                cols = slice(0, HALF)
+            acc3, acc4 = sums[e, g]
+            c3, s3 = w3q[a, g]
+            for i in range(2):
+                t = 2 * g + i
+                flags = dict(start=(a == 0 and i == 0), stop=(a == 1 and i == 1))
+                moving = dict(rhs=codes[:, cols].bitcast(FP8X4), rhs_scale=scales[:, cols])
+                nc.tensor.matmul_mx(
+                    out=acc3[:, HALF * i : HALF * (i + 1)], lhsT=c3[:, P * i : P * (i + 1)].bitcast(FP8X4),
+                    lhsT_scale=s3[:, P * i : P * (i + 1)], **moving, **flags,
+                )
+                col = N * a + P * t
+                nc.tensor.matmul_mx(
+                    out=acc4[:, HALF * i : HALF * (i + 1)], lhsT=w4c[:, 2 * col : 2 * (col + P)].bitcast(FP4X4),
+                    lhsT_scale=w45s[:, col : col + P], **moving, **flags,
+                )
+
+        def larger(e, g):
+            acc3, acc4 = sums[e, g]
+            first = ring.tile([P, BLOCK], F32, name="first%d_%d" % (e, g), tag="first", bufs=2)
+            nc.scalar.copy(first[:], acc3[:])
+            big = ring.tile([P, BLOCK], F32, name="big%d_%d" % (e, g), tag="big", bufs=2)
+            nc.vector.tensor_tensor(big[:], acc4[:], first[:], ALU.max)
+            return big
+
+        def add_skip(e, g, big):
+            idx = pos1_t[:, 16 * e : 16 * (e + 1)]
+            for i in range(2):
+                t = 2 * g + i
+                nc.vector.tensor_tensor(
+                    bloom[t][:, HALF * e : HALF * (e + 1)], skip[t][:].indirect(idx),
+                    big[:, HALF * i : HALF * (i + 1)], ALU.add,
+                )
+
+        for g in range(2):
+            second_pass(0, g, 0)
+        z10 = interleave(nc.scalar.copy, prod1[0], "z10")
+        lefts = [pick_first(4, HALF, HALF), pick_first(5, HALF, HALF)]
+        pick_second(4, HALF, HALF, lefts[0], prod1[1])
+        zq[1, 0] = quantise(z10, "zq10")
+        for g in range(2):
+            second_pass(0, g, 1)
+        for g in range(2):
+            second_pass(1, g, 0)
+        for s in range(5, 8):
+            if s + 1 < 8:
+                lefts.append(pick_first(s + 1, HALF, HALF))
+            pick_second(s, HALF, HALF, lefts[s - 4], prod1[1])
+        z11 = interleave(nc.scalar.copy, prod1[1], "z11")
+        bigs = [larger(0, 0), larger(0, 1)]
+        add_skip(0, 0, bigs[0])
+        zq[1, 1] = quantise(z11, "zq11")
+        for g in range(2):
+            second_pass(1, g, 1)
+        add_skip(0, 1, bigs[1])
+        bigs = [larger(1, 0), larger(1, 1)]
+        y = held([P, 4, NCON], F32, "y")
+        out_rows = out_0.rearrange("(p t) j -> p t j", t=4)
+        for g in range(2):
+            add_skip(1, g, bigs[g])
+        for g in range(2):
+            others = []
+            for i in range(2):
+                other = ring.tile([P, NCON], F32, name="other%d_%d" % (g, i), tag="other", bufs=2)
+                nc.vector.tensor_copy(other[:], bloom[2 * g + i][:].indirect(pos4_t[:]))
+                others.append(other)
+            for i in range(2):
+                t = 2 * g + i
+                nc.vector.tensor_tensor(y[:, t, :], bloom[t][:].indirect(pos3_t[:]), others[i][:], ALU.subtract)
+            nc.sync.dma_start(out_rows[:, 2 * g : 2 * g + 2, :], y[:, 2 * g : 2 * g + 2, :])
+
+        yc, ys = quantise(interleave(nc.vector.tensor_copy, y, "yb"), "yq")
+        nc.sync.dma_start(out_1[0].rearrange("p m t -> p (m t)").bitcast(I32), yc[:].bitcast(I32))
+        rows = out_2[0].bitcast(I32)
+        for q in range(4):
+            queue = nc.scalar if q % 2 else nc.sync
+            queue.dma_start(rows[4 * q : 4 * q + 4, :], ys[32 * q : 32 * q + 4, :].bitcast(I32))

@@ -88,26 +88,24 @@ def tile_list_bloom_bay_contrast_kernel(
             )
             return out
 
+        w2s_raw = held([P, H], U8, "w2s_raw", "stage_c")
+        nc.gpsimd.memset(w2s_raw[:].bitcast(I32), 0)
+        tabs = held([P, T], U8, "tabs")
+        nc.vector.memset(tabs[:].bitcast(I32), 0)
         offs_t = load_list(offs, "offs_t")
-        pos1_t = load_list(pos1, "pos1_t")
-        pos2_t = load_list(pos2, "pos2_t")
-        pos3_t = load_list(pos3, "pos3_t")
+        gain_t = held([P, 2, 4], F32, "gain_t", "stage_d")
+        nc.sync.dma_start(gain_t[:], gain.rearrange("(b p t) -> p b t", p=P, t=4))
+        load_scale_rows(nc.sync, w2s_raw, w2_scales, 0)
         w2_raw = held([P, 2 * H], U8, "w2_raw", "stage_a")
         nc.sync.dma_start(w2_raw[:].bitcast(I32), w2_words[0].bitcast(I32))
         w1_raw = [load_rows(w1[:, 0:BLOCK], "w1_raw0", "stage_b")]
+        load_scale_rows(nc.sync, tabs, tab_scales, 0)
         tabw = held([P, T], U32, "tabw")
         nc.sync.dma_start(tabw[:].bitcast(I32), tab_words[0].rearrange("p n i -> p (n i)").bitcast(I32))
+        pos1_t = load_list(pos1, "pos1_t")
+        pos2_t = load_list(pos2, "pos2_t")
+        pos3_t = load_list(pos3, "pos3_t")
         pos4_t = load_list(pos4, "pos4_t")
-
-        tabs = held([P, T], U8, "tabs")
-        nc.vector.memset(tabs[:].bitcast(I32), 0)
-        load_scale_rows(nc.scalar, tabs, tab_scales, 0)
-
-        gain_t = held([P, 2, 4], F32, "gain_t", "stage_d")
-        nc.gpsimd.dma_start(gain_t[:], gain.rearrange("(b p t) -> p b t", p=P, t=4))
-        w2s_raw = held([P, H], U8, "w2s_raw", "stage_c")
-        nc.gpsimd.memset(w2s_raw[:].bitcast(I32), 0)
-        load_scale_rows(nc.gpsimd, w2s_raw, w2_scales, 0)
 
         widths = (NPAIR, HALF)
         gain2 = []
@@ -116,6 +114,8 @@ def tile_list_bloom_bay_contrast_kernel(
             nc.scalar.activation(g[:], gain_t[:, b, :].unsqueeze(2).to_broadcast([P, 4, widths[b]]), ACT.Square)
             gain2.append(g)
 
+        w2s = held([P, H], U8, "w2s")
+        deal(w2s[:], w2s_raw[:])
         w2c = held([P, 2 * H], U8, "w2c")
         deal(w2c[:].bitcast(U16), w2_raw[:].bitcast(U16))
         w1q = {}
@@ -125,8 +125,6 @@ def tile_list_bloom_bay_contrast_kernel(
 
         vs = held([P, S], U8, "vs")
         nc.vector.tensor_copy(vs[:], tabs[:].indirect(offs_t[:]))
-        w2s = held([P, H], U8, "w2s")
-        deal(w2s[:], w2s_raw[:])
         vw = []
         for c in range(2):
             v = held([P, BLOCK], U32, "vw%d" % c)

@@ -1,6 +1,7 @@
 from contextlib import ExitStack
 
 import concourse.mybir as mybir
+from concourse.masks import make_identity
 
 K, T, S, NPAIR, NCON, H, N = 512, 4096, 1024, 512, 256, 1024, 512
 FLOPS = 2 * (2 * K * H * S + 2 * H * N * NPAIR + K * N * S)
@@ -65,7 +66,7 @@ def tile_list_bloom_bay_contrast_kernel(
             )
 
         def round_weight(copy, raw, pair, name):
-            out = ring.tile([P, 2 * BLOCK], BF16, name=name, tag="rounded", bufs=3, align_bytes=64)
+            out = ring.tile([P, 2 * BLOCK], BF16, name=name, tag="rounded", bufs=4, align_bytes=64)
             copy(
                 out[:].rearrange("p (t m j) -> p m t j", t=2, j=4),
                 raw[:].rearrange("p j (m t) -> p m t j", t=4)[:, :, 2 * pair : 2 * pair + 2, :],
@@ -84,7 +85,7 @@ def tile_list_bloom_bay_contrast_kernel(
             out = held([P, 4 * cols], BF16, name)
             copy(
                 out[:].rearrange("p (c i t) -> p c t i", i=4, t=4),
-                src[:].rearrange("p t (c i) -> p c t i", i=4),
+                src.rearrange("p t (c i) -> p c t i", i=4),
             )
             return out
 
@@ -109,10 +110,12 @@ def tile_list_bloom_bay_contrast_kernel(
 
         widths = (NPAIR, HALF)
         gain2 = []
-        for b in range(2):
-            g = held([P, 4, widths[b]], F32, "gain2_%d" % b)
-            nc.scalar.activation(g[:], gain_t[:, b, :].unsqueeze(2).to_broadcast([P, 4, widths[b]]), ACT.Square)
+        for b, count in enumerate((4, 2)):
+            g = held([P, count, widths[b]], F32, "gain2_%d" % b)
+            nc.scalar.activation(g[:], gain_t[:, b, 0:count].unsqueeze(2).to_broadcast([P, count, widths[b]]), ACT.Square)
             gain2.append(g)
+        gain_keep = held([P, 2], F32, "gain_keep")
+        nc.scalar.copy(gain_keep[:], gain_t[:, 1, 2:4])
 
         w2s = held([P, H], U8, "w2s")
         deal(w2s[:], w2s_raw[:])
@@ -153,6 +156,8 @@ def tile_list_bloom_bay_contrast_kernel(
 
         u = [held([P, S], F32, "u%d" % s) for s in range(8)]
         pending = {}
+        left = {}
+        prod = [held([P, 4, NPAIR], F32, "prod%d" % b) for b in range(2)]
 
         def first_products(s, c):
             b, t = divmod(s, 4)
@@ -162,24 +167,73 @@ def tile_list_bloom_bay_contrast_kernel(
             table_product(acc1, codes[:, cols].bitcast(FP8X4), scales[:, cols], c)
             acc2 = bank(2 + 2 * (s % 2) + c, "acc2_%d_%d" % (s, c))
             table_product(acc2, w2c[:, 2 * P * s : 2 * P * (s + 1)].bitcast(FP4X4), w2s[:, P * s : P * (s + 1)], c)
-            bent = ring.tile([P, BLOCK], F32, name="bent%d_%d" % (s, c), tag="bent", bufs=4)
-            nc.scalar.activation(bent[:], acc1[:], ACT.Tanh)
+            if c == 1 and s > 0:
+                bent = prod[(s - 1) // 4][:, (s - 1) % 4, :]
+            else:
+                left[s - 1, c] = ring.tile([P, BLOCK], F32, name="left%d_%d" % (s, c), tag="left", bufs=4)
+                bent = left[s - 1, c][:]
+            nc.scalar.activation(bent, acc1[:], ACT.Tanh)
             pending[s, c] = (acc2, bent)
 
         def add_products(s, c):
             acc2, bent = pending[s, c]
-            nc.vector.tensor_tensor(u[s][:, BLOCK * c : BLOCK * (c + 1)], acc2[:], bent[:], ALU.add)
+            nc.vector.tensor_tensor(u[s][:, BLOCK * c : BLOCK * (c + 1)], acc2[:], bent, ALU.add)
 
         def pick_first(s, first, count):
             b, t = divmod(s, 4)
-            a = ring.tile([P, count], F32, name="left%d_%d" % (s, first), tag="left", bufs=2)
+            if first == 0 and s < 5:
+                a = left[s, 0][:, 0:count]
+            else:
+                fresh = ring.tile([P, count], F32, name="fresh%d_%d" % (s, first), tag="fresh", bufs=3)
+                a = fresh[:]
             idx = pos1_t[:, first // 16 : (first + count) // 16]
-            nc.vector.tensor_tensor(a[:], u[s][:].indirect(idx), gain2[b][:, t, :], ALU.mult)
+            if s < 6:
+                nc.vector.tensor_tensor(a, u[s][:].indirect(idx), gain2[b][:, t, :], ALU.mult)
+            else:
+                nc.vector.tensor_copy(a, u[s][:].indirect(idx))
             return a
 
-        def pick_second(s, first, count, a, prod):
+        def pick_second(s, first, count, a):
             idx = pos2_t[:, first // 16 : (first + count) // 16]
-            nc.vector.tensor_tensor(prod[:, s % 4, :], u[s][:].indirect(idx), a[:], ALU.mult)
+            nc.vector.tensor_tensor(prod[s // 4][:, s % 4, first : first + count], u[s][:].indirect(idx), a, ALU.mult)
+
+        ident = held([P, P], F32, "ident")
+        make_identity(nc, ident[:])
+        turned = {}
+
+        def turned_products(jj):
+            codes, scales = w1q[1, 1]
+            acc1 = bank(6, "tacc1_%d" % jj)
+            acc2 = bank(7, "tacc2_%d" % jj)
+            for i in range(2):
+                c, j0 = divmod(256 * jj + P * i, BLOCK)
+                table = dict(
+                    lhsT=vw[c][:, j0 : j0 + P].bitcast(FP8X4), lhsT_scale=vs[:, BLOCK * c + j0 : BLOCK * c + j0 + P],
+                    start=True, stop=True,
+                )
+                nc.tensor.matmul_mx(out=acc1[:, 256 * i : 256 * (i + 1)], rhs=codes[:].bitcast(FP8X4), rhs_scale=scales[:], **table)
+                nc.tensor.matmul_mx(
+                    out=acc2[:, 256 * i : 256 * (i + 1)], rhs=w2c[:, 2 * P * 6 : 2 * P * 8].bitcast(FP4X4),
+                    rhs_scale=w2s[:, P * 6 : P * 8], **table,
+                )
+            bent = held([P, BLOCK], F32, "tbent%d" % jj)
+            nc.scalar.activation(bent[:], acc1[:], ACT.Tanh)
+            plain = held([P, BLOCK], F32, "tplain%d" % jj)
+            nc.scalar.copy(plain[:], acc2[:])
+            turned[jj] = (bent, plain)
+
+        def turn_back(s, c):
+            acc = bank(c, "back%d_%d" % (s, c))
+            for q in range(4):
+                jj, i = divmod(4 * c + q, 2)
+                cols = slice(256 * i + P * (s - 6), 256 * i + P * (s - 5))
+                for n, term in enumerate(turned[jj]):
+                    nc.tensor.matmul(
+                        acc[:, P * q : P * (q + 1)], term[:, cols], ident[:], start=(n == 0), stop=(n == 1), is_transpose=True
+                    )
+            nc.scalar.activation(
+                u[s][:, BLOCK * c : BLOCK * (c + 1)], acc[:], ACT.Copy, scale=gain_keep[:, s - 6 : s - 5]
+            )
 
         skip = [held([P, S], F32, "skip%d" % t) for t in range(4)]
         w5c = held([P, N], U32, "w5c")
@@ -201,8 +255,6 @@ def tile_list_bloom_bay_contrast_kernel(
                 nc.scalar.copy(skip[t][:, BLOCK * c : BLOCK * (c + 1)], acc[:])
 
         w3q = {}
-        prod0 = held([P, 4, NPAIR], F32, "prod0")
-        prod1 = [held([P, 4, HALF], F32, "prod1_%d" % e) for e in range(2)]
         zq = {}
 
         first_products(0, 0)
@@ -215,30 +267,41 @@ def tile_list_bloom_bay_contrast_kernel(
         for s in range(8):
             b = s // 4
             a = pick_first(s, 0, widths[b])
-            if s + 1 < 8:
+            if s + 1 < 6:
                 add_products(s + 1, 1)
-            if s + 2 < 8:
+            if s + 2 < 6:
                 first_products(s + 2, 0)
                 first_products(s + 2, 1)
-            pick_second(s, 0, widths[b], a, prod0 if b == 0 else prod1[0])
-            if s + 2 < 8:
+            if s < 5:
+                pick_second(s, 0, widths[b], a)
+            else:
+                if s > 5:
+                    pick_second(s - 1, 0, HALF, last)
+                last = a
+            if s + 2 < 6:
                 add_products(s + 2, 0)
             if s == 0:
                 r0 = round_weight(nc.scalar.copy, w1_raw[1], 0, "w1r10")
                 r1 = round_weight(nc.scalar.copy, w1_raw[1], 1, "w1r11")
                 w1q[1, 0] = quantise(r0, "w1q10")
                 w1q[1, 1] = quantise(r1, "w1q11")
+            if s in (1, 2):
+                turned_products(2 * s - 2)
+                turned_products(2 * s - 1)
             if s == 1:
                 deal_w45()
-            if 2 <= s < 6:
-                e = s - 2
-                w3q[divmod(e, 2)] = quantise(
-                    round_weight(nc.scalar.copy, w3_raw[e // 2], e % 2, "w3r%d" % e), "w3q%d" % e
-                )
-                skip_product(e)
             if s == 3:
-                z0 = interleave(nc.scalar.copy, prod0, "z0")
-            if s == 4:
+                for back in (6, 7):
+                    turn_back(back, 0)
+                    turn_back(back, 1)
+                w3r = []
+                for e in range(4):
+                    w3r.append(round_weight(nc.scalar.copy, w3_raw[e // 2], e % 2, "w3r%d" % e))
+                    skip_product(e)
+                z0 = interleave(nc.scalar.copy, prod[0][:], "z0")
+            if s >= 4:
+                w3q[divmod(s - 4, 2)] = quantise(w3r[s - 4], "w3q%d" % (s - 4))
+            if s == 7:
                 zq[0] = quantise(z0, "zq0")
 
         bloom = [held([P, NPAIR], F32, "bloom%d" % t) for t in range(4)]
@@ -271,7 +334,10 @@ def tile_list_bloom_bay_contrast_kernel(
 
         def larger(e, g):
             acc3, acc4 = sums[e, g]
-            first = ring.tile([P, BLOCK], F32, name="first%d_%d" % (e, g), tag="first", bufs=2)
+            if (e, g) == (0, 1):
+                first = held([P, BLOCK], F32, "first0_1", "prod1")
+            else:
+                first = ring.tile([P, BLOCK], F32, name="first%d_%d" % (e, g), tag="first", bufs=2)
             nc.scalar.copy(first[:], acc3[:])
             big = ring.tile([P, BLOCK], F32, name="big%d_%d" % (e, g), tag="big", bufs=2)
             nc.vector.tensor_tensor(big[:], acc4[:], first[:], ALU.max)
@@ -288,9 +354,11 @@ def tile_list_bloom_bay_contrast_kernel(
 
         for g in range(2):
             second_pass(0, g, 0)
-        z10 = interleave(nc.scalar.copy, prod1[0], "z10")
-        lefts = [pick_first(4, HALF, HALF), pick_first(5, HALF, HALF)]
-        pick_second(4, HALF, HALF, lefts[0], prod1[1])
+        lefts = [pick_first(4, HALF, HALF)]
+        pick_second(7, 0, HALF, last)
+        z10 = interleave(nc.scalar.copy, prod[1][:, :, 0:HALF], "z10")
+        lefts.append(pick_first(5, HALF, HALF))
+        pick_second(4, HALF, HALF, lefts[0])
         zq[1, 0] = quantise(z10, "zq10")
         for g in range(2):
             second_pass(0, g, 1)
@@ -299,16 +367,16 @@ def tile_list_bloom_bay_contrast_kernel(
         for s in range(5, 8):
             if s + 1 < 8:
                 lefts.append(pick_first(s + 1, HALF, HALF))
-            pick_second(s, HALF, HALF, lefts[s - 4], prod1[1])
-        z11 = interleave(nc.scalar.copy, prod1[1], "z11")
-        bigs = [larger(0, 0), larger(0, 1)]
-        add_skip(0, 0, bigs[0])
+            pick_second(s, HALF, HALF, lefts[s - 4])
+        z11 = interleave(nc.scalar.copy, prod[1][:, :, HALF:NPAIR], "z11")
+        add_skip(0, 0, larger(0, 0))
         zq[1, 1] = quantise(z11, "zq11")
         for g in range(2):
             second_pass(1, g, 1)
-        add_skip(0, 1, bigs[1])
+        add_skip(0, 1, larger(0, 1))
         bigs = [larger(1, 0), larger(1, 1)]
         y = held([P, 4, NCON], F32, "y")
+        yb = held([P, 4 * NCON], BF16, "yb")
         out_rows = out_0.rearrange("(p t) j -> p t j", t=4)
         for g in range(2):
             add_skip(1, g, bigs[g])
@@ -322,8 +390,13 @@ def tile_list_bloom_bay_contrast_kernel(
                 t = 2 * g + i
                 nc.vector.tensor_tensor(y[:, t, :], bloom[t][:].indirect(pos3_t[:]), others[i][:], ALU.subtract)
             nc.sync.dma_start(out_rows[:, 2 * g : 2 * g + 2, :], y[:, 2 * g : 2 * g + 2, :])
+            copy = nc.vector.tensor_copy if g else nc.scalar.copy
+            copy(
+                yb[:].rearrange("p (c i t) -> p c t i", i=4, t=4)[:, :, 2 * g : 2 * g + 2, :],
+                y[:, 2 * g : 2 * g + 2, :].rearrange("p t (c i) -> p c t i", i=4),
+            )
 
-        yc, ys = quantise(interleave(nc.vector.tensor_copy, y, "yb"), "yq")
+        yc, ys = quantise(yb, "yq")
         nc.sync.dma_start(out_1[0].rearrange("p m t -> p (m t)").bitcast(I32), yc[:].bitcast(I32))
         rows = out_2[0].bitcast(I32)
         for q in range(4):

from contextlib import ExitStack

import concourse.mybir as mybir
from concourse.masks import make_identity

K, T, S, NPAIR, NCON, H, N = 512, 4096, 1024, 512, 256, 1024, 512
FLOPS = 2 * (2 * K * H * S + 2 * H * N * NPAIR + K * N * S)

F32 = mybir.dt.float32
BF16 = mybir.dt.bfloat16
I32 = mybir.dt.int32
U32 = mybir.dt.uint32
U16 = mybir.dt.uint16
U8 = mybir.dt.uint8
FP8X4 = mybir.dt.float8_e4m3fn_x4
FP4X4 = mybir.dt.float4_e2m1fn_x4
ALU = mybir.AluOpType
ACT = mybir.ActivationFunctionType

P = 128
BLOCK = 512
HALF = NPAIR // 2


def tile_list_bloom_bay_contrast_kernel(
    tc, tab_words, tab_scales, offs, pos1, pos2, pos3, pos4, w1, w2_words, w2_scales, gain, w3,
    w4_words, w4_scales, w5_words, w5_scales, out_0, out_1, out_2,
):
    nc = tc.nc
    with ExitStack() as ctx:
        lists = ctx.enter_context(tc.tile_pool(name="lists", bufs=1))
        keep = ctx.enter_context(tc.tile_pool(name="keep", bufs=1))
        ring = ctx.enter_context(tc.tile_pool(name="ring", bufs=2))
        psum = ctx.enter_context(tc.psum_pool(name="psum", bufs=1))

        def held(shape, dtype, name, tag=None):
            return keep.tile(shape, dtype, name=name, tag=tag or name, align_bytes=64)

        def bank(i, name):
            return psum.tile([P, BLOCK], F32, name=name, tag="bank%d" % i)

        def load_list(src, name):
            tile = lists.tile(list(src.shape), U16, name=name)
            nc.sync.dma_start(tile[:], src)
            return tile

        def load_scale_rows(queue, tile, src, first_row):
            passes, cols = src.shape[0], src.shape[2]
            rows = src.bitcast(I32)
            for q in range(4):
                dst = tile[32 * q + first_row : 32 * q + first_row + 4, 0 : passes * cols].bitcast(I32)
                queue.dma_start(
                    dst.rearrange("r (a c) -> r a c", a=passes),
                    rows[:, 4 * q : 4 * q + 4, :].rearrange("a r c -> r a c"),
                )

        def load_rows(src, name, tag):
            tile = held([P, 4, BLOCK], F32, name, tag)
            nc.sync.dma_start(tile[:], src.rearrange("(p j) c -> p j c", j=4))
            return tile

        def deal(dst, src):
            nc.vector.tensor_copy(
                dst.rearrange("p (b t m) -> p b t m", t=4, m=P),
                src.rearrange("p (b m t) -> p b t m", t=4, m=P),
            )

        def round_weight(copy, raw, pair, name):
            out = ring.tile([P, 2 * BLOCK], BF16, name=name, tag="rounded", bufs=4, align_bytes=64)
            copy(
                out[:].rearrange("p (t m j) -> p m t j", t=2, j=4),
                raw[:].rearrange("p j (m t) -> p m t j", t=4)[:, :, 2 * pair : 2 * pair + 2, :],
            )
            return out

        def quantise(src, name):
            cols = src.shape[1] // 4
            codes = held([P, cols], U32, name + "_codes")
            scales = held([P, cols], U8, name + "_scales")
            nc.vector.quantize_mx(out=codes[:].bitcast(FP8X4), scales=scales[:], in_=src[:])
            return codes, scales

        def interleave(copy, src, name):
            cols = src.shape[2]
            out = held([P, 4 * cols], BF16, name)
            copy(
                out[:].rearrange("p (c i t) -> p c t i", i=4, t=4),
                src.rearrange("p t (c i) -> p c t i", i=4),
            )
            return out

        w2s_raw = held([P, H], U8, "w2s_raw", "stage_c")
        nc.gpsimd.memset(w2s_raw[:].bitcast(I32), 0)
        tabs = held([P, T], U8, "tabs")
        nc.vector.memset(tabs[:].bitcast(I32), 0)
        offs_t = load_list(offs, "offs_t")
        gain_t = held([P, 2, 4], F32, "gain_t", "stage_d")
        nc.sync.dma_start(gain_t[:], gain.rearrange("(b p t) -> p b t", p=P, t=4))
        load_scale_rows(nc.sync, w2s_raw, w2_scales, 0)
        w2_raw = held([P, 2 * H], U8, "w2_raw", "stage_a")
        nc.sync.dma_start(w2_raw[:].bitcast(I32), w2_words[0].bitcast(I32))
        w1_raw = [load_rows(w1[:, 0:BLOCK], "w1_raw0", "stage_b")]
        load_scale_rows(nc.sync, tabs, tab_scales, 0)
        tabw = held([P, T], U32, "tabw")
        nc.sync.dma_start(tabw[:].bitcast(I32), tab_words[0].rearrange("p n i -> p (n i)").bitcast(I32))
        pos1_t = load_list(pos1, "pos1_t")
        pos2_t = load_list(pos2, "pos2_t")
        pos3_t = load_list(pos3, "pos3_t")
        pos4_t = load_list(pos4, "pos4_t")

        widths = (NPAIR, HALF)
        gain2 = []
        for b, count in enumerate((4, 2)):
            g = held([P, count, widths[b]], F32, "gain2_%d" % b)
            nc.scalar.activation(g[:], gain_t[:, b, 0:count].unsqueeze(2).to_broadcast([P, count, widths[b]]), ACT.Square)
            gain2.append(g)
        gain_keep = held([P, 2], F32, "gain_keep")
        nc.scalar.copy(gain_keep[:], gain_t[:, 1, 2:4])

        w2s = held([P, H], U8, "w2s")
        deal(w2s[:], w2s_raw[:])
        w2c = held([P, 2 * H], U8, "w2c")
        deal(w2c[:].bitcast(U16), w2_raw[:].bitcast(U16))
        w1q = {}
        r0 = round_weight(nc.vector.tensor_copy, w1_raw[0], 0, "w1r00")
        r1 = round_weight(nc.scalar.copy, w1_raw[0], 1, "w1r01")
        w1q[0, 0] = quantise(r0, "w1q00")

        vs = held([P, S], U8, "vs")
        nc.vector.tensor_copy(vs[:], tabs[:].indirect(offs_t[:]))
        vw = []
        for c in range(2):
            v = held([P, BLOCK], U32, "vw%d" % c)
            nc.vector.tensor_copy(v[:], tabw[:].indirect(offs_t[:, 32 * c : 32 * (c + 1)]))
            vw.append(v)
        w1q[0, 1] = quantise(r1, "w1q01")

        w1_raw.append(load_rows(w1[:, BLOCK:H], "w1_raw1", "stage_a"))
        w45_raw = held([P, 4 * N + 4 * N], U8, "w45_raw", "stage_d")
        nc.sync.dma_start(w45_raw[:, 0 : 4 * N].bitcast(I32), w5_words[0].rearrange("p n i -> p (n i)").bitcast(I32))
        nc.sync.dma_start(
            w45_raw[:, 4 * N : 8 * N].bitcast(I32).rearrange("p (a c) -> p a c", a=2),
            w4_words.bitcast(I32).rearrange("a p c -> p a c"),
        )
        w45s_raw = held([P, 2 * N], U8, "w45s_raw", "stage_c")
        nc.gpsimd.memset(w45s_raw[:].bitcast(I32), 0)
        load_scale_rows(nc.sync, w45s_raw, w5_scales, 4)
        load_scale_rows(nc.sync, w45s_raw, w4_scales, 0)
        w3_raw = [load_rows(w3[0:BLOCK, :], "w3_raw0", "stage_b"), load_rows(w3[BLOCK:H, :], "w3_raw1", "stage_a")]

        def table_product(out, codes, scales, c):
            nc.tensor.matmul_mx(
                out=out[:], lhsT=codes, lhsT_scale=scales, rhs=vw[c][:].bitcast(FP8X4),
                rhs_scale=vs[:, BLOCK * c : BLOCK * (c + 1)], start=True, stop=True,
            )

        u = [held([P, S], F32, "u%d" % s) for s in range(8)]
        pending = {}
        left = {}
        prod = [held([P, 4, NPAIR], F32, "prod%d" % b) for b in range(2)]

        def first_products(s, c):
            b, t = divmod(s, 4)
            codes, scales = w1q[b, t // 2]
            cols = slice(P * (t % 2), P * (t % 2 + 1))
            acc1 = bank(c, "acc1_%d_%d" % (s, c))
            table_product(acc1, codes[:, cols].bitcast(FP8X4), scales[:, cols], c)
            acc2 = bank(2 + 2 * (s % 2) + c, "acc2_%d_%d" % (s, c))
            table_product(acc2, w2c[:, 2 * P * s : 2 * P * (s + 1)].bitcast(FP4X4), w2s[:, P * s : P * (s + 1)], c)
            if c == 1 and s > 0:
                bent = prod[(s - 1) // 4][:, (s - 1) % 4, :]
            else:
                left[s - 1, c] = ring.tile([P, BLOCK], F32, name="left%d_%d" % (s, c), tag="left", bufs=4)
                bent = left[s - 1, c][:]
            nc.scalar.activation(bent, acc1[:], ACT.Tanh)
            pending[s, c] = (acc2, bent)

        def add_products(s, c):
            acc2, bent = pending[s, c]
            nc.vector.tensor_tensor(u[s][:, BLOCK * c : BLOCK * (c + 1)], acc2[:], bent, ALU.add)

        def pick_first(s, first, count):
            b, t = divmod(s, 4)
            if first == 0 and s < 5:
                a = left[s, 0][:, 0:count]
            else:
                fresh = ring.tile([P, count], F32, name="fresh%d_%d" % (s, first), tag="fresh", bufs=3)
                a = fresh[:]
            idx = pos1_t[:, first // 16 : (first + count) // 16]
            if s < 6:
                nc.vector.tensor_tensor(a, u[s][:].indirect(idx), gain2[b][:, t, :], ALU.mult)
            else:
                nc.vector.tensor_copy(a, u[s][:].indirect(idx))
            return a

        def pick_second(s, first, count, a):
            idx = pos2_t[:, first // 16 : (first + count) // 16]
            nc.vector.tensor_tensor(prod[s // 4][:, s % 4, first : first + count], u[s][:].indirect(idx), a, ALU.mult)

        ident = held([P, P], F32, "ident")
        make_identity(nc, ident[:])
        turned = {}

        def turned_products(jj):
            codes, scales = w1q[1, 1]
            acc1 = bank(6, "tacc1_%d" % jj)
            acc2 = bank(7, "tacc2_%d" % jj)
            for i in range(2):
                c, j0 = divmod(256 * jj + P * i, BLOCK)
                table = dict(
                    lhsT=vw[c][:, j0 : j0 + P].bitcast(FP8X4), lhsT_scale=vs[:, BLOCK * c + j0 : BLOCK * c + j0 + P],
                    start=True, stop=True,
                )
                nc.tensor.matmul_mx(out=acc1[:, 256 * i : 256 * (i + 1)], rhs=codes[:].bitcast(FP8X4), rhs_scale=scales[:], **table)
                nc.tensor.matmul_mx(
                    out=acc2[:, 256 * i : 256 * (i + 1)], rhs=w2c[:, 2 * P * 6 : 2 * P * 8].bitcast(FP4X4),
                    rhs_scale=w2s[:, P * 6 : P * 8], **table,
                )
            bent = held([P, BLOCK], F32, "tbent%d" % jj)
            nc.scalar.activation(bent[:], acc1[:], ACT.Tanh)
            plain = held([P, BLOCK], F32, "tplain%d" % jj)
            nc.scalar.copy(plain[:], acc2[:])
            turned[jj] = (bent, plain)

        def turn_back(s, c):
            acc = bank(c, "back%d_%d" % (s, c))
            for q in range(4):
                jj, i = divmod(4 * c + q, 2)
                cols = slice(256 * i + P * (s - 6), 256 * i + P * (s - 5))
                for n, term in enumerate(turned[jj]):
                    nc.tensor.matmul(
                        acc[:, P * q : P * (q + 1)], term[:, cols], ident[:], start=(n == 0), stop=(n == 1), is_transpose=True
                    )
            nc.scalar.activation(
                u[s][:, BLOCK * c : BLOCK * (c + 1)], acc[:], ACT.Copy, scale=gain_keep[:, s - 6 : s - 5]
            )

        skip = [held([P, S], F32, "skip%d" % t) for t in range(4)]
        w5c = held([P, N], U32, "w5c")
        w4c = held([P, 4 * N], U8, "w4c")
        w45s = held([P, 2 * N], U8, "w45s")

        def deal_w45():
            nc.vector.tensor_copy(
                w5c[:].bitcast(I32).rearrange("p (t q i) -> p q t i", t=4, i=4),
                w45_raw[:, 0 : 4 * N].bitcast(I32).rearrange("p (q i t) -> p q t i", t=4, i=4),
            )
            deal(w45s[:], w45s_raw[:])
            deal(w4c[:].bitcast(U16), w45_raw[:, 4 * N : 8 * N].bitcast(U16))

        def skip_product(t):
            for c in range(2):
                acc = bank(6 + c, "acc5_%d_%d" % (t, c))
                table_product(acc, w5c[:, P * t : P * (t + 1)].bitcast(FP8X4), w45s[4:P, P * t : P * (t + 1)], c)
                nc.scalar.copy(skip[t][:, BLOCK * c : BLOCK * (c + 1)], acc[:])

        w3q = {}
        zq = {}

        first_products(0, 0)
        first_products(0, 1)
        add_products(0, 0)
        first_products(1, 0)
        add_products(0, 1)
        first_products(1, 1)
        add_products(1, 0)
        for s in range(8):
            b = s // 4
            a = pick_first(s, 0, widths[b])
            if s + 1 < 6:
                add_products(s + 1, 1)
            if s + 2 < 6:
                first_products(s + 2, 0)
                first_products(s + 2, 1)
            if s < 5:
                pick_second(s, 0, widths[b], a)
            else:
                if s > 5:
                    pick_second(s - 1, 0, HALF, last)
                last = a
            if s + 2 < 6:
                add_products(s + 2, 0)
            if s == 0:
                r0 = round_weight(nc.scalar.copy, w1_raw[1], 0, "w1r10")
                r1 = round_weight(nc.scalar.copy, w1_raw[1], 1, "w1r11")
                w1q[1, 0] = quantise(r0, "w1q10")
                w1q[1, 1] = quantise(r1, "w1q11")
            if s in (1, 2):
                turned_products(2 * s - 2)
                turned_products(2 * s - 1)
            if s == 1:
                deal_w45()
            if s == 3:
                for back in (6, 7):
                    turn_back(back, 0)
                    turn_back(back, 1)
                w3r = []
                for e in range(4):
                    w3r.append(round_weight(nc.scalar.copy, w3_raw[e // 2], e % 2, "w3r%d" % e))
                    skip_product(e)
                z0 = interleave(nc.scalar.copy, prod[0][:], "z0")
            if s >= 4:
                w3q[divmod(s - 4, 2)] = quantise(w3r[s - 4], "w3q%d" % (s - 4))
            if s == 7:
                zq[0] = quantise(z0, "zq0")

        bloom = [held([P, NPAIR], F32, "bloom%d" % t) for t in range(4)]
        sums = {}
        banks_of = ((6, 7, 0, 1), (2, 3, 4, 5))

        def second_pass(e, g, a):
            if a == 0:
                sums[e, g] = (bank(banks_of[e][g], "acc3_%d_%d" % (e, g)), bank(banks_of[e][2 + g], "acc4_%d_%d" % (e, g)))
                codes, scales = zq[0]
                cols = slice(HALF * e, HALF * (e + 1))
            else:
                codes, scales = zq[1, e]
                cols = slice(0, HALF)
            acc3, acc4 = sums[e, g]
            c3, s3 = w3q[a, g]
            for i in range(2):
                t = 2 * g + i
                flags = dict(start=(a == 0 and i == 0), stop=(a == 1 and i == 1))
                moving = dict(rhs=codes[:, cols].bitcast(FP8X4), rhs_scale=scales[:, cols])
                nc.tensor.matmul_mx(
                    out=acc3[:, HALF * i : HALF * (i + 1)], lhsT=c3[:, P * i : P * (i + 1)].bitcast(FP8X4),
                    lhsT_scale=s3[:, P * i : P * (i + 1)], **moving, **flags,
                )
                col = N * a + P * t
                nc.tensor.matmul_mx(
                    out=acc4[:, HALF * i : HALF * (i + 1)], lhsT=w4c[:, 2 * col : 2 * (col + P)].bitcast(FP4X4),
                    lhsT_scale=w45s[:, col : col + P], **moving, **flags,
                )

        def larger(e, g):
            acc3, acc4 = sums[e, g]
            if (e, g) == (0, 1):
                first = held([P, BLOCK], F32, "first0_1", "prod1")
            else:
                first = ring.tile([P, BLOCK], F32, name="first%d_%d" % (e, g), tag="first", bufs=2)
            nc.scalar.copy(first[:], acc3[:])
            big = ring.tile([P, BLOCK], F32, name="big%d_%d" % (e, g), tag="big", bufs=2)
            nc.vector.tensor_tensor(big[:], acc4[:], first[:], ALU.max)
            return big

        def add_skip(e, g, big):
            idx = pos1_t[:, 16 * e : 16 * (e + 1)]
            for i in range(2):
                t = 2 * g + i
                nc.vector.tensor_tensor(
                    bloom[t][:, HALF * e : HALF * (e + 1)], skip[t][:].indirect(idx),
                    big[:, HALF * i : HALF * (i + 1)], ALU.add,
                )

        for g in range(2):
            second_pass(0, g, 0)
        lefts = [pick_first(4, HALF, HALF)]
        pick_second(7, 0, HALF, last)
        z10 = interleave(nc.scalar.copy, prod[1][:, :, 0:HALF], "z10")
        lefts.append(pick_first(5, HALF, HALF))
        pick_second(4, HALF, HALF, lefts[0])
        zq[1, 0] = quantise(z10, "zq10")
        for g in range(2):
            second_pass(0, g, 1)
        for g in range(2):
            second_pass(1, g, 0)
        for s in range(5, 8):
            if s + 1 < 8:
                lefts.append(pick_first(s + 1, HALF, HALF))
            pick_second(s, HALF, HALF, lefts[s - 4])
        z11 = interleave(nc.scalar.copy, prod[1][:, :, HALF:NPAIR], "z11")
        add_skip(0, 0, larger(0, 0))
        zq[1, 1] = quantise(z11, "zq11")
        for g in range(2):
            second_pass(1, g, 1)
        add_skip(0, 1, larger(0, 1))
        bigs = [larger(1, 0), larger(1, 1)]
        y = held([P, 4, NCON], F32, "y")
        yb = held([P, 4 * NCON], BF16, "yb")
        out_rows = out_0.rearrange("(p t) j -> p t j", t=4)
        for g in range(2):
            add_skip(1, g, bigs[g])
        for g in range(2):
            others = []
            for i in range(2):
                other = ring.tile([P, NCON], F32, name="other%d_%d" % (g, i), tag="other", bufs=2)
                nc.vector.tensor_copy(other[:], bloom[2 * g + i][:].indirect(pos4_t[:]))
                others.append(other)
            for i in range(2):
                t = 2 * g + i
                nc.vector.tensor_tensor(y[:, t, :], bloom[t][:].indirect(pos3_t[:]), others[i][:], ALU.subtract)
            nc.sync.dma_start(out_rows[:, 2 * g : 2 * g + 2, :], y[:, 2 * g : 2 * g + 2, :])
            copy = nc.vector.tensor_copy if g else nc.scalar.copy
            copy(
                yb[:].rearrange("p (c i t) -> p c t i", i=4, t=4)[:, :, 2 * g : 2 * g + 2, :],
                y[:, 2 * g : 2 * g + 2, :].rearrange("p t (c i) -> p c t i", i=4),
            )

        yc, ys = quantise(yb, "yq")
        nc.sync.dma_start(out_1[0].rearrange("p m t -> p (m t)").bitcast(I32), yc[:].bitcast(I32))
        rows = out_2[0].bitcast(I32)
        for q in range(4):
            queue = nc.scalar if q % 2 else nc.sync
            queue.dma_start(rows[4 * q : 4 * q + 4, :], ys[32 * q : 32 * q + 4, :].bitcast(I32))
